import numpy as np
import ml_dtypes

BF16 = ml_dtypes.bfloat16


def bf(x):
    return np.asarray(x, np.float32).astype(BF16)


def f32(x):
    return np.asarray(x, np.float32)


def f64(x):
    return np.asarray(x).astype(np.float64)


def striped(idx):
    return np.concatenate([l.reshape(-1, 16).T for l in idx])


def rows(idx, k):
    return np.tile(np.repeat(idx, 16, axis=0), (k // (16 * 8), 1))


def look(tab, idx):
    return np.take_along_axis(f64(tab), rows(idx, len(tab)), axis=1)


K, S, V, N = 512, 2048, 1024, 1024


def setup_inputs():
    return {"tab": f32(0.5 * np.random.standard_normal((K, S))), "y": f32(np.random.standard_normal((K, V))), "offs": striped(np.stack([np.random.permutation(S)[:N] for _ in range(8)]))}


def reference(tab, y, offs):
    idx = np.stack([g.T.reshape(-1) for g in np.split(offs, 8)])
    t = look(tab, idx)
    x = np.exp(t) * f64(y)
    return x

@@ -1,0 +1,43 @@
+import concourse.mybir as mybir
+
+F32 = mybir.dt.float32
+U16 = mybir.dt.uint16
+EXP = mybir.ActivationFunctionType.Exp
+MULT = mybir.AluOpType.mult
+
+P = 128
+LANES = 16
+PIECE = 512
+
+BYTES = 4 * (512 * 2048 + 512 * 1024 + 512 * 1024) + 2 * (128 * 64)
+
+
+def tile_lookup_gate_exp_out_kernel(tc, tab, y, offs, out):
+    nc = tc.nc
+    rows, columns = tab.shape
+    entries = y.shape[1]
+    blocks = rows // P
+    piece_columns = PIECE // LANES
+
+    with (
+        tc.tile_pool(name="lists", bufs=1) as lists,
+        tc.tile_pool(name="work", bufs=blocks) as work,
+    ):
+        offsets = lists.tile([P, entries // LANES], U16, name="offsets")
+        nc.sync.dma_start(offsets[:], offs)
+
+        for b in range(blocks):
+            block = slice(b * P, (b + 1) * P)
+            table = work.tile([P, columns], F32, name="table")
+            stream = work.tile([P, entries], F32, name="stream")
+            gate = work.tile([P, entries], F32, name="gate")
+            product = work.tile([P, entries], F32, name="product")
+
+            nc.sync.dma_start(table[:], tab[block, :])
+            nc.sync.dma_start(stream[:], y[block, :])
+            for k in range(entries // PIECE):
+                piece = slice(k * PIECE, (k + 1) * PIECE)
+                listed = offsets[:, k * piece_columns : (k + 1) * piece_columns]
+                nc.scalar.activation(gate[:, piece], table[:].indirect(listed), EXP)
+                nc.vector.tensor_tensor(product[:, piece], gate[:, piece], stream[:, piece], MULT)
+            nc.sync.dma_start(out[block, :], product[:])

@@ -19,25 +19,23 @@ def tile_lookup_gate_exp_out_kernel(tc, tab, y, offs, out):
     blocks = rows // P
     piece_columns = PIECE // LANES
 
-    with (
-        tc.tile_pool(name="lists", bufs=1) as lists,
-        tc.tile_pool(name="work", bufs=blocks) as work,
-    ):
-        offsets = lists.tile([P, entries // LANES], U16, name="offsets")
+    with tc.tile_pool(name="held", bufs=1) as held:
+        offsets = held.tile([P, entries // LANES], U16, name="offsets")
         nc.sync.dma_start(offsets[:], offs)
 
+        tables = [held.tile([P, columns], F32, name=f"table{b}") for b in range(blocks)]
+        streams = [held.tile([P, entries], F32, name=f"stream{b}") for b in range(blocks)]
         for b in range(blocks):
-            block = slice(b * P, (b + 1) * P)
-            table = work.tile([P, columns], F32, name="table")
-            stream = work.tile([P, entries], F32, name="stream")
-            gate = work.tile([P, entries], F32, name="gate")
-            product = work.tile([P, entries], F32, name="product")
+            nc.sync.dma_start(tables[b][:], tab[b * P : (b + 1) * P, :])
+        for b in range(blocks):
+            nc.sync.dma_start(streams[b][:], y[b * P : (b + 1) * P, :])
 
-            nc.sync.dma_start(table[:], tab[block, :])
-            nc.sync.dma_start(stream[:], y[block, :])
+        for b in range(blocks):
+            gate = held.tile([P, entries], F32, name=f"gate{b}")
+            product = held.tile([P, entries], F32, name=f"product{b}")
             for k in range(entries // PIECE):
                 piece = slice(k * PIECE, (k + 1) * PIECE)
                 listed = offsets[:, k * piece_columns : (k + 1) * piece_columns]
-                nc.scalar.activation(gate[:, piece], table[:].indirect(listed), EXP)
-                nc.vector.tensor_tensor(product[:, piece], gate[:, piece], stream[:, piece], MULT)
-            nc.sync.dma_start(out[block, :], product[:])
+                nc.scalar.activation(gate[:, piece], tables[b][:].indirect(listed), EXP)
+                nc.vector.tensor_tensor(product[:, piece], gate[:, piece], streams[b][:, piece], MULT)
+            nc.sync.dma_start(out[b * P : (b + 1) * P, :], product[:])

@@ -25,6 +25,7 @@ def tile_lookup_gate_exp_out_kernel(tc, tab, y, offs, out):
 
         tables = [held.tile([P, columns], F32, name=f"table{b}") for b in range(blocks)]
         streams = [held.tile([P, entries], F32, name=f"stream{b}") for b in range(blocks)]
+        products = [held.tile([P, entries], F32, name=f"product{b}") for b in range(blocks)]
         for b in range(blocks):
             nc.sync.dma_start(tables[b][:], tab[b * P : (b + 1) * P, :])
         for b in range(blocks):
@@ -32,10 +33,12 @@ def tile_lookup_gate_exp_out_kernel(tc, tab, y, offs, out):
 
         for b in range(blocks):
             gate = held.tile([P, entries], F32, name=f"gate{b}")
-            product = held.tile([P, entries], F32, name=f"product{b}")
             for k in range(entries // PIECE):
                 piece = slice(k * PIECE, (k + 1) * PIECE)
                 listed = offsets[:, k * piece_columns : (k + 1) * piece_columns]
                 nc.scalar.activation(gate[:, piece], tables[b][:].indirect(listed), EXP)
-                nc.vector.tensor_tensor(product[:, piece], gate[:, piece], streams[b][:, piece], MULT)
-            nc.sync.dma_start(out[b * P : (b + 1) * P, :], product[:])
+                nc.vector.tensor_tensor(products[b][:, piece], gate[:, piece], streams[b][:, piece], MULT)
+
+        for b in range(blocks):
+            queue = nc.sync if b % 2 == 0 else nc.scalar
+            queue.dma_start(out[b * P : (b + 1) * P, :], products[b][:])

import concourse.mybir as mybir

F32 = mybir.dt.float32
U16 = mybir.dt.uint16
EXP = mybir.ActivationFunctionType.Exp
MULT = mybir.AluOpType.mult

P = 128
LANES = 16
PIECE = 512

BYTES = 4 * (512 * 2048 + 512 * 1024 + 512 * 1024) + 2 * (128 * 64)


def tile_lookup_gate_exp_out_kernel(tc, tab, y, offs, out):
    nc = tc.nc
    rows, columns = tab.shape
    entries = y.shape[1]
    blocks = rows // P
    piece_columns = PIECE // LANES

    with tc.tile_pool(name="held", bufs=1) as held:
        offsets = held.tile([P, entries // LANES], U16, name="offsets")
        nc.sync.dma_start(offsets[:], offs)

        tables = [held.tile([P, columns], F32, name=f"table{b}") for b in range(blocks)]
        streams = [held.tile([P, entries], F32, name=f"stream{b}") for b in range(blocks)]
        products = [held.tile([P, entries], F32, name=f"product{b}") for b in range(blocks)]
        for b in range(blocks):
            nc.sync.dma_start(tables[b][:], tab[b * P : (b + 1) * P, :])
        for b in range(blocks):
            nc.sync.dma_start(streams[b][:], y[b * P : (b + 1) * P, :])

        for b in range(blocks):
            gate = held.tile([P, entries], F32, name=f"gate{b}")
            for k in range(entries // PIECE):
                piece = slice(k * PIECE, (k + 1) * PIECE)
                listed = offsets[:, k * piece_columns : (k + 1) * piece_columns]
                nc.scalar.activation(gate[:, piece], tables[b][:].indirect(listed), EXP)
                nc.vector.tensor_tensor(products[b][:, piece], gate[:, piece], streams[b][:, piece], MULT)

        for b in range(blocks):
            queue = nc.sync if b % 2 == 0 else nc.scalar
            queue.dma_start(out[b * P : (b + 1) * P, :], products[b][:])
